import numpy as np, ml_dtypes
CORES = [3,11,19,27,35,43,51,59]
N = 8
BF = ml_dtypes.bfloat16
def gentries(a):
    return np.ascontiguousarray(a.reshape(8, 16, -1).transpose(0, 2, 1)).reshape(8, -1)
def gtable(e):
    e = np.asarray(e); return np.ascontiguousarray(e.reshape(8, -1, 16).transpose(0, 2, 1)).reshape(128, -1).astype(np.int32)
R, M, L, F, RO = 256, 768, 2, 512, 3
V = R + L * M
AT = [0] + [R + i * M for i in range(L + 1)]
LEV = np.repeat(np.arange(L + 1), np.diff(AT))
TOP = np.concatenate([2 * np.array(AT)[LEV[R:]], np.full(R, 2 * V)])
LOW = np.array(AT)[LEV + 1]
def under(rng, shape, top):
    return np.minimum((rng.random(shape) * top).astype(np.int64), np.asarray(top) - 1)
def parts(rng):
    i = np.arange(16)[:, None]; sh = (N, 8, 1, V)
    p = rng.integers(0, 16, sh); p2 = (p + rng.integers(1, 16, sh)) % 16
    t = 1 + (255 * rng.random(sh) ** (1.5 + LEV)).astype(np.int64); t2 = 1 + (255 * rng.random(sh) ** (1.5 + LEV)).astype(np.int64)
    x = np.where(i == p, t, 0); x = np.where((i == p2) & (rng.random(sh) < 0.125), t2, x); x = np.where(rng.random(sh) < 0.02, 0, x)
    s = (256 * rng.random((N, 8, 16, R)) ** 1.5).astype(np.int64)
    c = rng.integers(0, 256, (N, 8, 16, R + F)) * (rng.random((N, 8, 16, R + F)) > 0.15)
    half = rng.random(sh) < 0.75
    o = np.argsort(rng.random((N, 8, 16, V)) + 10 * (half & (i >= 8)), axis=2)
    k = np.where(half, rng.choice(np.array([0, 1, 1, 2, 2, 3, 4, 8]), sh), rng.choice(np.array([1, 2, 3, 5, 12, 16]), sh))
    e = np.where(o < k, under(rng, (N, 8, 16, V), TOP), 2 * V)
    a = LOW + under(rng, (N, 8, 2, V), V + R + F - LOW)
    return x, s, c[..., :R].copy(), c[..., R:].copy(), e, a
def rich(rng, x, v):
    k = rng.integers(3, 17, (N, 8, 1, V)); o = np.argsort(rng.random(x.shape), axis=2)
    return np.where(rng.random((N, 8, 1, V)) < 0.25, np.where(o < k, v, 0), x)
def pack(x, s, q, c, e, a):
    def b(v):
        return np.ascontiguousarray(v.reshape(N, 128, -1)).astype(np.float32).astype(BF)
    return {"piv": b(x), "safe": b(s), "lem": b(q), "leaf": b(c), "uses": np.ascontiguousarray(e.reshape(N, 128, V)).astype(np.int32), "prem": np.stack([gtable(v) for v in a.reshape(N, 8, 2 * V)])}
def setup_inputs(rng):
    return pack(*parts(rng))
def setup_inputs_turn(rng):
    x, s, q, c, e, a = parts(rng); i = np.arange(16)[:, None]
    j = rng.integers(0, 16, (N, 8, 1, 1)); w = rng.integers(0, 7, (N, 8, 1, V))
    w[..., :7] = np.arange(7)
    one, two = i == j, i == (j + 8) % 16
    m = np.where(w == 0, one, np.where(w == 1, two, np.where(w == 2, one | two, np.where(w == 3, i < 8, np.where(w == 4, i >= 8, w == 5)))))
    n = under(rng, (N, 8, 16, V), TOP); n = n - (n & 1) * (rng.random(n.shape) < 0.5)
    x = np.where(rng.random((N, 8, 1, V)) < 0.3, 0, x)
    return pack(x, s, q, c, np.where(m, n, 2 * V), a)
def setup_inputs_ties(rng):
    x, s, q, c, e, a = parts(rng); v = np.array([0, 1, 127, 128, 129, 254, 255])
    x = rich(rng, x, 1)
    x = np.where(x > 0, rng.choice(np.array([1, 127, 128, 129, 255]), x.shape), 0); nx = np.roll(x, 8, axis=2)
    s, q, c = rng.choice(v, s.shape), rng.choice(v, q.shape), rng.choice(v, c.shape)
    s[..., 0] = x[..., 0]; s[..., 1] = np.maximum(x[..., 1] - 1, 0); s[..., 2] = np.maximum(x[..., 2], nx[..., 2]); s[..., 3] = nx[..., 3]
    return pack(x, s, q, c, e, a)
def setup_inputs_alike(rng):
    x, s, q, c, e, a = parts(rng); on = e < 2 * V
    e[:, 1] = np.where(on[:, 1], under(rng, (N, 1, V), TOP), 2 * V)
    e[:, 2] = np.where(on[:, 2], np.where(rng.random((N, 16, V)) < 0.5, 0, TOP - 1), 2 * V)
    e[:, 3] = 2 * V
    e[:, 4] = np.where(on[:, 4], TOP - 1 - rng.integers(0, 16, (N, 16, V)), 2 * V)
    e[:, 5] = under(rng, (N, 16, V), TOP)
    a[:, 1, 1] = a[:, 1, 0]; a[:, 2] = np.where(rng.random((N, 2, V)) < 0.5, LOW, V + R + F - 1)
    a[:, 4] = V + rng.integers(0, R, (N, 2, V)); a[:, 5] = V + R + rng.integers(0, F, (N, 2, V)); a[:, 6] = LOW
    return pack(x, s, q, c, e, a)
def setup_inputs_late(rng):
    x, s, q, c, e, a = parts(rng); g = int(rng.integers(0, 8)); s[:] = 0
    q2, c2 = rng.integers(200, 256, q.shape), rng.integers(200, 256, c.shape); q2[:, g] = q[:, g]; c2[:, g] = c[:, g]
    e[..., V - R:] = np.where(rng.random((N, 8, 1, R)) < 0.5, 2 * V, e[..., V - R:])
    return pack(x, s, q2, c2, e, a)
def setup_inputs_spread(rng):
    x, s, q, c, e, a = parts(rng)
    def u(n):
        return np.minimum((np.exp2(8 * rng.random((N, 8, 1, n))) * rng.random((N, 8, 16, n))).astype(np.int64), 255)
    x = np.where(x > 0, np.minimum(np.exp2(8 * rng.random(x.shape)).astype(np.int64), 255), 0)
    x = rich(rng, x, np.maximum(u(V), 1))
    m = rng.random((N, 8, 16, V)) < rng.random((N, 8, 1, V)) ** 3
    return pack(x, u(R), u(R), u(F), np.where(m, under(rng, (N, 8, 16, V), TOP), 2 * V), a)
def check_inputs(d):
    bad = []
    for k in ("piv", "safe", "lem", "leaf"):
        v = np.asarray(d[k]).astype(np.float32)
        if not np.all((v >= 0) & (v <= 255) & (v == np.floor(v))): bad.append("whole numbers from 0 to 255 in " + k)
    e = np.asarray(d["uses"]).astype(np.int64)
    if not np.all(((e >= 0) & (e < TOP)) | (e == 2 * V)): bad.append("range of uses")
    a = np.stack([gentries(v) for v in d["prem"]]).astype(np.int64).reshape(N, 8, 2, V)
    if not np.all((a >= LOW) & (a < V + R + F)): bad.append("range of prem")
    return bad
def least(S, e):
    return np.stack([[np.min(np.take(S[q, g], e[q, g], axis=1), axis=1) for g in range(8)] for q in range(N)])
def splice(e, st):
    K = np.zeros((N, 8, 1, 2 * V + 1), bool)
    K[:, :, 0, 2 * R:2 * V:2] = st[..., R:] == 1; K[:, :, 0, 2 * R + 1:2 * V:2] = st[..., R:] == 2
    loose = np.take_along_axis(K, e, 3); has = np.any(loose, axis=2, keepdims=True); j = np.argmax(loose, axis=2)[:, :, None]
    this = (np.arange(16)[:, None] == j) & has
    u = np.take_along_axis(e, j, 2) >> 1
    t = np.roll(np.take_along_axis(e, np.where(has, u - R, 0), 3), 8, axis=2)
    hit = np.any((t != 2 * V) & (e != 2 * V) & ~this, axis=2, keepdims=True)
    return np.where(has & ~hit, np.where(t != 2 * V, t, np.where(this, 2 * V, e)), e)
def reference(piv, safe, lem, leaf, uses, prem):
    def w(v):
        return v.astype(np.float32).astype(np.int64).reshape(N, 8, 16, -1)
    x = w(piv); nx = np.roll(x, 8, axis=2)
    s = np.full((N, 8, 16, V), 255, np.int64); s[..., :R] = w(safe)
    C = np.zeros((N, 8, 16, V + R + F), np.int64); C[..., V:V + R] = w(lem); C[..., V + R:] = w(leaf)
    e = uses.astype(np.int64).reshape(N, 8, 16, V)
    a = np.stack([gentries(v) for v in prem]).astype(np.int64).reshape(N, 8, 2, V)
    st = np.zeros((N, 8, V), np.int64); S = np.full((N, 8, 16, 2 * V + 1), 255, np.int64); gs = None
    for rnd in range(RO):
        old = st[:, :, None] > 0
        if rnd:
            s[..., :R] = np.where(old[..., :R], s[..., :R], np.roll(gs, 1, axis=0))
            C[..., V:V + R] = np.roll(C[..., :R], -1, axis=0)
            e = splice(e, st)
        for l in range(L + 1):
            i, j = AT[l], AT[l + 1]
            if l: s[..., i:j] = np.where(old[..., i:j], s[..., i:j], least(S, e[..., i - R:j - R]))
            y, p, n = s[..., i:j], x[..., i:j], nx[..., i:j]; b = st[..., i:j]
            b = np.where(b > 0, b, np.where(np.all(y >= p, axis=2), 1, np.where(np.all(y >= n, axis=2), 2, 0)))
            st[..., i:j] = b; b = b[:, :, None]
            S[..., 2 * i:2 * j:2] = np.where(b == 0, np.maximum(y, p), np.where(b == 1, y, 255))
            S[..., 2 * i + 1:2 * j:2] = np.where(b == 0, np.maximum(y, n), np.where(b == 2, y, 255))
        gs = least(S, e[..., V - R:])
        for l in range(L, -1, -1):
            i, j = AT[l], AT[l + 1]; p, n = x[..., i:j], nx[..., i:j]; b = st[..., i:j]
            A = np.take_along_axis(C, a[:, :, :1, i:j], 3); B = np.take_along_axis(C, a[:, :, 1:, i:j], 3)
            b = np.where(b > 0, b, np.where(~np.all(A >= p, axis=2), 1, np.where(~np.all(B >= n, axis=2), 2, 0)))
            st[..., i:j] = b; b = b[:, :, None]
            C[..., i:j] = np.where(b == 1, A, np.where(b == 2, B, np.maximum(np.where(p > 0, 0, A), np.where(n > 0, 0, B))))
    return {"yc": np.ascontiguousarray(C[..., :V]).reshape(N, 128, V).astype(np.float32).astype(BF), "ys": np.concatenate([s, gs], axis=3).reshape(N, 128, V + R).astype(np.float32).astype(BF)}

from concourse.mybir import AluOpType as A, AxisListType, ActivationFunctionType as AF

R, M, V, F, RO = 256, 768, 1792, 512, 3
E = 2 * V
W = 256
U = 64
BF, F4, I4, U2 = "bfloat16", "float32", "int32", "uint16"

SCRATCH = {}


def _b(name, n, d=BF):
    SCRATCH[name] = ("sbuf", [128, n], d)


for _n in ("one", "I", "tb", "ON", "PM", "t1", "t2", "LO", "HI", "E0", "E8", "g1", "g2", "GA", "GB", "QA", "QB", "QF", "HA", "HB", "NB", "PB", "JN", "ksi"):
    _b(_n, 128)
_b("P32", 128, F4); _b("J32", 128, F4); _b("sela", 2048, F4); _b("pw", 1, F4)
_b("R1", 32 * U); _b("R2", 32 * U)
_b("x", V); _b("s", V); _b("ui", V, I4); _b("pi", 224, I4); _b("po", 224, U2)
_b("ou", V, U2); _b("ov1", 1024, U2); _b("ov2", 1024, U2)
_b("lt0", 1552, F4); _b("lt1", 1552, F4); _b("lg0", 256, F4); _b("lg1", 256, F4)
_b("S1", 528); _b("S2", 3600); _b("S3", 3600); _b("K2", 3600); _b("K3", 3600)
for _r in range(RO):
    _b("C%d" % _r, V + R + F); _b("sa%d" % _r, R); _b("gs%d" % _r, R)
_b("ga", 16 * M); _b("sc", 16 * M); _b("kg", 16 * 384); _b("ks", 16 * M)
_b("fd", V); _b("dm", V)
for _i in range(3):
    _b("v%d" % _i, 512); _b("z%d" % _i, 512); _b("ab%d" % _i, 512); _b("tm%d" % _i, 256)
_b("th", 1024); _b("P", 1024, F4); _b("tg", 1024, F4); _b("lm", 1024); _b("hm", 1024); _b("ch", 1024); _b("nl", 1024, F4)
_b("w1", 64, I4); _b("w2", 64, I4); _b("wu", 64, U2)
BANKS = ["b%d" % _i for _i in range(8)]
for _n in BANKS:
    SCRATCH[_n] = ("psum", [128, 512], F4)
ND = 64
SEMAPHORES = ["eV", "eS", "eP", "eG"] + ["d%d" % _i for _i in range(ND)] + ["%s%d" % (_p, _r) for _p in ("ra", "rb", "la", "lb") for _r in range(RO - 1)]
EXT = {"piv": BF, "safe": BF, "lem": BF, "leaf": BF, "uses": I4, "prem": I4, "yc": BF, "ys": BF}

CYC, XLAT = 0.83, 150.0
PEN, SLACK, FAC = 8000.0, 150.0, (0.6, 0.7)


def _psum(v):
    return v[0] in BANKS


def _two(v):
    return (SCRATCH[v[0]][2] if v[0] in SCRATCH else EXT[v[0]]) in (BF, U2)


def _hi(v):
    return v[1] + (v[2] - 1) * v[3] + 1


def _over(a, b):
    if a[0] >= b[1] or b[0] >= a[1]:
        return False
    return not (a[2] == b[2] and a[2] > 1 and (a[0] - b[0]) % a[2])


def _covers(a, b):
    return a[0] <= b[0] and a[1] >= b[1] and (a[2] == 1 or (a[2] == b[2] and (a[0] - b[0]) % a[2] == 0))


def _program():
    ops, bufs, last, nd = [], {}, {}, [0]

    def add(kind, engs, cost, reads, writes, **kw):
        i = len(ops)
        preds = {}
        for v in reads:
            reg = (v[1], _hi(v), v[3]); b = bufs.setdefault(v[0], {"w": [], "r": []})
            for (q, j) in b["w"]:
                if _over(q, reg):
                    preds[j] = True
        for v in writes:
            reg = (v[1], _hi(v), v[3]); b = bufs.setdefault(v[0], {"w": [], "r": []})
            for (q, j) in b["w"]:
                if _over(q, reg):
                    preds[j] = True
            for (q, j) in b["r"]:
                if _over(q, reg):
                    preds.setdefault(j, False)
        for v in list(reads) + list(writes):
            if _psum(v) and v[0] in last and last[v[0]] != i:
                preds.setdefault(last[v[0]], None)
        for v in list(reads) + list(writes):
            if _psum(v):
                last[v[0]] = i
        preds.pop(i, None)
        for v in writes:
            reg = (v[1], _hi(v), v[3]); b = bufs[v[0]]
            b["w"] = [z for z in b["w"] if not _covers(reg, z[0])] + [(reg, i)]
            b["r"] = [z for z in b["r"] if not _covers(reg, z[0])]
        for v in reads:
            bufs[v[0]]["r"].append(((v[1], _hi(v), v[3]), i))
        op = {"kind": kind, "engs": engs, "cost": cost, "preds": preds, "id": i, "lat": 0.0, "sem": None}
        op.update(kw)
        ops.append(op)
        return i

    def c(name, lo, n, st=1):
        return (name, lo, n, st)

    def all_(name):
        return (name, 0, SCRATCH[name][1][1], 1)

    def dma(out, in_):
        k = nd[0]; nd[0] += 1
        n = max(out[2], in_[2]) * (2 if _two(out) else 4)
        add("dma", ("Y",), 60.0, [in_], [out], out=out, in_=in_, lat=2000.0 + n * 128 / 150.0, sem=("d%d" % k, 16))

    def memset(out, val):
        add("memset", ("V",), 60 + out[2] * CYC * (.5 if _two(out) else 1), [], [out], out=out, val=val)

    def tt(out, a, b, op):
        add("tt", ("V",), 60 + out[2] * CYC * (1 if _psum(a) or _psum(b) else 2), [a, b], [out], out=out, a=a, b=b, op=op)

    def _fast(out, a):
        return .5 if _two(out) and _two(a) and not _psum(a) else 1

    def ts(out, a, s1, op0, s2=None, op1=None):
        rd = [a] + ([s1] if isinstance(s1, tuple) else [])
        add("ts", ("V",), 60 + out[2] * CYC * _fast(out, a), rd, [out], out=out, a=a, s1=s1, s2=s2, op0=op0, op1=op1)

    def vcopy(out, a):
        add("vcopy", ("V",), 60 + out[2] * CYC * _fast(out, a), [a], [out], out=out, a=a)

    def act(out, a, func, scale=1.0, bias=0.0):
        add("act", ("S",), 70 + out[2] * CYC, [a], [out], out=out, a=a, func=func, scale=scale, bias=bias)

    def either(out, a, func, scale, bias, s1, op0, s2=None, op1=None):
        add("either", ("S", "V"), 70 + out[2] * CYC, [a], [out], out=out, a=a, func=func, scale=scale, bias=bias, s1=s1, op0=op0, s2=s2, op1=op1)

    def ecopy(out, a):
        add("ecopy", ("S", "V"), 65 + out[2] * CYC, [a], [out], out=out, a=a)

    def scan(out, d0, d1, op0, op1):
        add("scan", ("V",), 60 + out[2] * CYC * .5, [d0, d1], [out], out=out, d0=d0, d1=d1, op0=op0, op1=op1)

    def gather(out, win, off):
        add("gather", ("S", "V"), 60 + out[2] * CYC * 1.5, [win, off], [out], out=out, win=win, off=off)

    def mm(out, lhs, rhs, start, stop, fp=False):
        add("mm", ("P",), 30 + max(64, out[2]) * .75 * (4 if fp else 1), [lhs, rhs], [out], out=out, lhs=lhs, rhs=rhs, start=start, stop=stop)

    def group(out, terms, fp=False):
        for k, (l, r) in enumerate(terms):
            mm(out, all_(l), r, k == 0, k == len(terms) - 1, fp)

    def asel(out, in_, pat, op, base, cm):
        add("asel", ("G",), 170 + out[2] * CYC * 2, [in_], [out], out=out, in_=in_, pat=pat, op=op, base=base, cm=cm)

    def fill(out, val):
        add("iota", ("G",), 130 + out[2] * CYC * 2, [], [out], out=out, val=val)

    dma(c("s", 0, R), c("safe", 0, R))
    dma(c("x", 0, R), c("piv", 0, R))
    dma(c("ui", 0, M), c("uses", 0, M))
    dma(c("x", R, V - R), c("piv", R, V - R))
    dma(c("ui", M, 1024), c("uses", M, 1024))
    dma(all_("pi"), c("prem", 0, 224))
    dma(c("C0", V, R), c("lem", 0, R))
    for r in range(RO):
        dma(c("C%d" % r, V + R, F), c("leaf", 0, F))
    memset(all_("one"), 1.0)
    asel(all_("I"), all_("one"), [[-1, 128]], A.is_equal, 0, 1)
    asel(all_("tb"), all_("one"), [[-16, 8], [0, 16]], A.is_ge, 0, 1)
    asel(all_("ON"), all_("tb"), [[16, 8], [0, 16]], A.is_ge, 15, -1)
    asel(all_("t1"), all_("ON"), [[-1, 128]], A.is_equal, -8, 1)
    asel(all_("t2"), all_("ON"), [[-1, 128]], A.is_equal, 8, 1)
    tt(all_("PM"), all_("t1"), all_("t2"), A.add)

    def half(out, in_, h):
        asel(all_(out), all_(in_), [[0, 8], [1, 2], [0, 8]], A.is_equal, -h, 0)

    def mix(out, a, b):
        ts(all_("g1"), all_("E0"), float(a), A.mult)
        ts(all_("g2"), all_("E8"), float(b), A.mult)
        tt(all_(out), all_("g1"), all_("g2"), A.add)
    half("LO", "ON", 0)
    half("HI", "ON", 1)
    asel(all_("E0"), all_("ON"), [[-16, 8], [0, 16]], A.is_equal, 0, 1)
    asel(all_("E8"), all_("ON"), [[-16, 8], [0, 16]], A.is_equal, -8, 1)
    mix("GA", -2048, 1024)
    ts(all_("GB"), all_("GA"), -1.0, A.mult)
    tt(all_("QB"), all_("HI"), all_("LO"), A.subtract)
    ts(all_("QA"), all_("QB"), -32.0, A.mult)
    half("t1", "GA", 0)
    half("t2", "GA", 1)
    tt(all_("QF"), all_("t2"), all_("t1"), A.subtract)
    mix("HA", -256, 256)
    ts(all_("HB"), all_("HA"), -1.0, A.mult)
    mix("PB", 128, 128)
    ts(all_("NB"), all_("PB"), -1.0, A.mult)
    ts(all_("JN"), all_("ON"), -1.0, A.mult)
    memset(all_("R1"), 0.0); memset(c("R1", 0, 2 * U, 16), 255.0)
    fill(c("S1", 512, 16), 255); fill(c("S2", 2048, 1552), 255); fill(c("S3", E, 16), 255)
    for k in range(3):
        ts(c("ou", k * W, W), c("ui", k * W, W), 512, A.min)
    for k in range(3, 7):
        vcopy(c("ou", k * W, W), c("ui", k * W, W))
    for n0, w, t in ((1024, 768, 1792), (256, 768, 1024), (0, 256, 256)):
        for h in (0, 112):
            k = h + n0 // 16
            ts(c("po", k, w // 16), c("pi", k, w // 16), -t, A.add)
    fill(c("K2", 0, 512), 0); fill(c("K2", 2048, 1552), 0); fill(c("K3", 0, 512), 0); fill(c("K3", E, 16), 0)

    def late():
        memset(all_("R2"), 2.0); memset(c("R2", 0, 2 * U, 16), 0.0)
        scan(all_("ksi"), c("R2", 0, 128), all_("I"), A.mult, A.max)
        add("red", ("V",), 80.0, [c("ksi", 15, 8, 16)], [all_("pw")], out=all_("pw"), a=c("ksi", 15, 8, 16))
        vcopy(all_("P32"), all_("PM"))
        ts(all_("J32"), all_("I"), -1.0, A.mult)
        fill(all_("sela"), 1)
        asel(all_("sela"), all_("sela"), [[1, 16], [0, 8], [-1, 16]], A.is_equal, 0, 0)
        asel(all_("sela"), all_("sela"), [[0, 16], [-16, 8], [0, 16]], A.is_ge, 0, 1)
        asel(all_("sela"), all_("sela"), [[0, 16], [16, 8], [0, 16]], A.is_ge, 15, -1)
        for k in range(6):
            ts(c("lt0", k * W, W), c("ui", k * W, W), -1.0, A.mult, float(E), A.add)
        ts(all_("lg0"), c("ui", 1536, W), -1.0, A.mult, float(E), A.add)
        memset(c("lt0", 1536, 16), 0.0); memset(c("lt1", 1536, 16), 0.0)
        dma(c("lt1", 0, M), c("lt0", 0, M))

    def lists(win, off, o0, n, gbuf, sbuf, g0, pat, op0, op1):
        size = SCRATCH[gbuf][1][1]
        for k in range(0, n, 2 * U):
            at = (g0 + k) * 16 % size
            for h in (0, U):
                gather(c(gbuf, at + 16 * h, 16 * U), win, c(off, o0 + k + h, U))
            scan(c(sbuf, (g0 + k) * 16, 32 * U), all_(pat), c(gbuf, at, 32 * U), op0, op1)

    def premises(r, n0, stream):
        lo = 256 if n0 < R else 1024 if n0 < 1024 else 1792
        win = c("C%d" % r, lo, V + R + F - lo)
        for h in (0, 1):
            gather(c("ab%d" % stream, h * W, W), win, c("po", 112 * h + n0 // 16, W // 16))

    def down(r, n0, stream, Mv):
        p, q = "b%d" % (2 * stream), "b%d" % (2 * stream + 1)
        x, s, v = c("x", n0, W), c("s", n0, W), "v%d" % stream
        if r:
            dm = c("dm", n0, W)
            group(c(q, 0, W), [("I", s), ("NB", dm)])
            group(c(q, W, W), [("I", s), ("PB", dm)])
            group(c(p, 0, W), [("I", x), ("HA", dm)])
            group(c(p, W, W), [("PM", x), ("HB", dm)])
            tm = c("tm%d" % stream, 0, W)
            tt(tm, Mv, c(q, 0, W), A.min)
            tt(s, tm, c(q, W, W), A.max)
        else:
            group(c(p, 0, W), [("I", x)])
            group(c(p, W, W), [("PM", x)])
            if Mv is not None:
                ecopy(s, Mv)
        tt(c(v, 0, W), s, c(p, 0, W), A.is_lt)
        tt(c(v, W, W), s, c(p, W, W), A.is_lt)
        group(c(q, 0, W), [("LO", c(v, 0, W)), ("HI", c(v, W, W))])
        if n0 >= 1024:
            premises(r, n0, stream)
            tt(c("z%d" % stream, 0, 2 * W), c("ab%d" % stream, 0, 2 * W), c(p, 0, 2 * W), A.is_lt)
        fd = c("fd", n0, W)
        either(fd, c(q, 0, W), AF.Relu, -1.0, 1.0, 0.0, A.is_equal)
        group(c(p, 0, W), [("I", x), ("GA", fd)])
        group(c(p, W, W), [("PM", x), ("GB", fd)])
        t = "S1" if n0 < R else "S2" if n0 < 1024 else "S3"
        tt(c(t, 2 * n0, W, 2), s, c(p, 0, W), A.max)
        tt(c(t, 2 * n0 + 1, W, 2), s, c(p, W, W), A.max)

    def up(r, n0, stream):
        p, q = "b%d" % (2 * stream), "b%d" % (2 * stream + 1)
        x, fd, dm = c("x", n0, W), c("fd", n0, W), c("dm", n0, W)
        ab, v, C = "ab%d" % stream, "v%d" % stream, "C%d" % r
        if n0 >= 1024:
            v = "z%d" % stream
        else:
            group(c(p, 0, W), [("I", x)])
            group(c(p, W, W), [("PM", x)])
            premises(r, n0, stream)
            tt(c(v, 0, 2 * W), c(ab, 0, 2 * W), c(p, 0, 2 * W), A.is_lt)
        group(c(q, 0, W), [("QA", c(v, 0, W)), ("QB", c(v, W, W)), ("QF", fd)])
        act(dm, c(q, 0, W), AF.Sign, 1.0, -0.5)
        group(c(p, 0, W), [("I", x), ("HA", dm)])
        group(c(p, W, W), [("PM", x), ("HB", dm)])
        if r < RO - 1 and n0 >= R:
            k = "K2" if n0 < 1024 else "K3"
            act(c(k, 2 * n0 + 1, W, 2), c(p, 0, W), AF.Sign, 1.0, -255.5)
            act(c(k, 2 * n0, W, 2), c(p, W, W), AF.Sign, 1.0, -255.5)
        either(c(p, 0, 2 * W), c(p, 0, 2 * W), AF.Relu, -1024.0, 512.0, 0.0, A.is_le, 512.0, A.mult)
        tm = c("tm%d" % stream, 0, W)
        tt(tm, c(ab, 0, W), c(p, 0, W), A.min)
        tt(c(p, W, W), c(ab, W, W), c(p, W, W), A.min)
        tt(c(C, n0, W), tm, c(p, W, W), A.max)
        if r == RO - 1:
            dma(c("yc", n0, W), c(C, n0, W))

    def kscan(r, part):
        off, o0 = ("ou", M) if r == 1 else ("ov1", 0)
        if part == 0:
            lists(all_("K2"), off, o0, M, "kg", "ks", 0, "R2", A.mult, A.max)
        else:
            lists(all_("K3"), off, o0 + M, R, "kg", "ks", 0, "R2", A.mult, A.max)

    def splice(r, part):
        lt, ov = "lt%d" % (r - 1), "ov%d" % r
        c0, n = (0, M) if part == 0 else (M, R)

        def L(k):
            return c(lt, M + k, W) if part == 0 else c("lg%d" % (r - 1), k, W)
        for k in range(0, n, W):
            ts(c("th", c0 + k, W), c("ks", 16 * k + 15, W, 16), all_("pw"), A.is_equal)
            tt(c("P", c0 + k, W), c("th", c0 + k, W), L(k), A.mult)
        w = c("b6", 0, n // 16); wo = c0 // 16; m = n // 16
        for q in range(16):
            mm(w, c("sela", 128 * q, 128), c("P", c0 + q, m, 16), q == 0, q == 15, True)
        ts(c("w1", wo, m), w, -1.0, A.mult, float(E - 512), A.add)
        ts(c("w2", wo, m), c("w1", wo, m), 1, A.arith_shift_right)
        vcopy(c("wu", wo, m), c("w2", wo, m))
        for k in range(0, n, W):
            gather(c("tg", c0 + k, W), all_(lt), c("wu", wo + k // 16, 16))
        for k in range(0, n, W):
            z = "b%d" % (7 - (k // W) % 2)
            P, lm, hm = c("P", c0 + k, W), c("lm", c0 + k, W), c("hm", c0 + k, W)
            group(c(z, 0, W), [("P32", c("tg", c0 + k, W)), ("J32", P)], fp=True)
            tt(lm, P, c(z, 0, W), A.min)
            tt(hm, L(k), c(z, 0, W), A.min)
            group(c(z, W, W), [("ON", hm), ("JN", lm)])
            either(c("ch", c0 + k, W), c(z, W, W), AF.Relu, -1.0, 1.0, 0.0, A.is_equal)
            tt(c("tg", c0 + k, W), c("ch", c0 + k, W), c(z, 0, W), A.mult)
            if r == 1:
                nl = c("lt1", M + k, W) if part == 0 else c("lg1", k, W)
            else:
                nl = c("nl", c0 + k, W)
            tt(nl, c("tg", c0 + k, W), L(k), A.add)
            ts(c(ov, c0 + k, W), nl, -1.0, A.mult, float(E), A.add)

    def send(src, dst, lo, to, rs, ls):
        j = add("send", ("G",), 300.0, [src], [], src=src, dst=dst, at=(lo, lo + R), to=to, rs=rs, lat=2500.0, sem=(ls, 8))
        add("arrive", ("R",), 0.0, [], [c(dst, lo, R)], lat=1000.0, sem=(rs, 8), after=j)

    for r in range(RO):
        off2, o2 = ("ou", M) if r == 0 else ("ov%d" % r, 0)
        if r:
            kscan(r, 0)
        down(r, 0, 0, None if r == 0 else all_("sa%d" % r))
        dma(c("S2", 0, 512), c("S1", 0, 512))
        if r:
            splice(r, 0)
        for k in range(3):
            lists(all_("S1"), "ou", k * W, W, "ga", "sc", k * W, "R1", A.max, A.min)
            down(r, R + k * W, (k + 1) % 3, c("sc", 16 * k * W + 15, W, 16))
        dma(c("S3", 0, 2048), c("S2", 0, 2048))
        if r == 0:
            late()
        else:
            kscan(r, 1)
            splice(r, 1)
        for k in range(3):
            lists(all_("S2"), off2, o2 + k * W, W, "ga", "sc", k * W, "R1", A.max, A.min)
            down(r, 1024 + k * W, k, c("sc", 16 * k * W + 15, W, 16))
        if r == RO - 1:
            for k in range(7):
                dma(c("ys", k * W, W), c("s", k * W, W))
        lists(all_("S3"), off2, o2 + M, R, "ga", "sc", 0, "R1", A.max, A.min)
        gs = all_("gs%d" % r)
        ecopy(gs, c("sc", 15, R, 16))
        if r < RO - 1:
            send(gs, "sa%d" % (r + 1), 0, 1, "ra%d" % r, "la%d" % r)
        else:
            dma(c("ys", V, R), gs)
        for k in range(3):
            up(r, 1024 + k * W, k)
        for k in range(3):
            up(r, R + k * W, k)
        if r < RO - 1:
            dma(c("K3", 512, 1536), c("K2", 512, 1536))
        up(r, 0, 0)
        if r < RO - 1:
            send(c("C%d" % r, 0, R), "C%d" % (r + 1), V, -1, "rb%d" % r, "lb%d" % r)
    return ops


def _schedule(ops):
    n = len(ops)
    for o in ops:
        if "after" in o:
            o["preds"].setdefault(o["after"], False)
    succ = [[] for _ in range(n)]
    left = [len(o["preds"]) for o in ops]
    for o in ops:
        for p in o["preds"]:
            succ[p].append(o["id"])
    rank = [0.0] * n
    for i in range(n - 1, -1, -1):
        o = ops[i]
        acc, best = 0.0, 0.0
        for j in sorted(succ[i], key=lambda j: -rank[j]):
            best = max(best, rank[j] + 100 + acc)
            acc += ops[j]["cost"] * FAC[ops[j]["kind"] == "gather"]
        rank[i] = o["cost"] + o["lat"] + best
    free = {"V": 0.0, "S": 0.0, "P": 0.0, "G": 0.0, "Y": 0.0, "R": 0.0}
    done, eng, order = [0.0] * n, [None] * n, []
    ready = [i for i in range(n) if left[i] == 0]
    while ready:
        cand, first = [], 1e18
        for i in ready:
            o = ops[i]
            for e in o["engs"]:
                t = free[e]
                for p, hard in o["preds"].items():
                    d = done[p]
                    if eng[p] != e or ops[p]["sem"]:
                        d += XLAT
                    elif hard is not None and e != "P":
                        d += 60.0
                    if d > t:
                        t = d
                cand.append((t, i, e))
                if t < first:
                    first = t
        best = None
        for t, i, e in cand:
            if t <= first + SLACK:
                pr = rank[i]
                if len(ops[i]["engs"]) > 1 and e == "V":
                    pr -= PEN if ops[i]["kind"] == "gather" else PEN * 0.3
                if best is None or pr > best[0] or (pr == best[0] and t < best[1]):
                    best = (pr, t, i, e)
        pr, t, i, e = best
        o = ops[i]
        eng[i] = e
        if e != "R":
            free[e] = t + o["cost"]
        done[i] = t + o["cost"] + o["lat"]
        order.append(i)
        ready.remove(i)
        for j in succ[i]:
            left[j] -= 1
            if left[j] == 0:
                ready.append(j)
    return order, eng, max(done)


def _waits(ops, order, eng):
    pos = {i: k for k, i in enumerate(order)}
    count = {"V": 0, "S": 0, "P": 0, "G": 0}
    know = {e: {} for e in "VSPGYR"}
    sem, clock, need, final, waited = {}, {}, {}, {}, {}
    for i in order:
        o, e = ops[i], eng[i]
        k = know[e]
        w = {}
        if e != "R":
            ps = [p for p, hard in o["preds"].items() if ops[p]["sem"] or eng[p] != e or (hard is not None and e != "P")]
            ps.sort(key=lambda p: -pos[p])
            for p in ps:
                s, val = sem[p]
                if k.get(s, 0) >= val:
                    continue
                w[s] = max(w.get(s, 0), val)
                k[s] = val
                for a, b in clock[p].items():
                    if k.get(a, 0) < b:
                        k[a] = b
        need[i] = sorted(w.items())
        for s, val in w.items():
            waited[s] = max(waited.get(s, 0), val)
        if o["sem"]:
            sem[i] = o["sem"]
        else:
            count[e] += 1
            sem[i] = ("e" + e, count[e])
        final[sem[i][0]] = max(final.get(sem[i][0], 0), sem[i][1])
        clock[i] = dict(k) if e != "R" else {}
    tail = [(s, v) for s, v in sorted(final.items()) if waited.get(s, 0) < v]
    return need, sem, tail


_PLAN = {}


def _plan():
    if not _PLAN:
        ops = _program()
        order, eng, est = _schedule(ops)
        need, sem, tail = _waits(ops, order, eng)
        _PLAN.update({"ops": ops, "order": order, "eng": eng, "need": need, "sem": sem, "tail": tail, "est": est})
    return _PLAN


def rank_program(g, core, T, topo):
    rank = T.rank_of(core)
    if rank is None:
        return
    pl = _plan()
    queue = {"V": g.vector, "S": g.scalar, "P": g.tensor, "G": g, "Y": g.sync}

    def ap(v):
        if v[3] == 1:
            return T[v[0]][:, v[1]:v[1] + v[2]]
        return T[v[0]][:, v[1]:_hi(v):v[3]]

    for i in pl["order"]:
        o, e = pl["ops"][i], pl["eng"][i]
        if e == "R":
            continue
        q = queue[e]
        for s, val in pl["need"][i]:
            q.wait_ge(T.sem[s], val)
        kind = o["kind"]
        s, val = pl["sem"][i]
        if kind == "send":
            dst = T.cores[(rank + o["to"]) % len(T.cores)]
            rid, pid, se = topo.addr(dst)
            g.remote_dma(out_ap=T[o["dst"]][:, o["at"][0]:o["at"][1]], in_ap=ap(o["src"]), remote_sem=T.sem[o["rs"]], local_sem=T.sem[s],
                         pid=pid, routing_id=rid, dma_engine_mask=topo.mask(core, dst))
            continue
        if kind == "dma":
            q.dma_start(out=ap(o["out"]), in_=ap(o["in_"])).then_inc(T.sem[s], 16)
            continue
        out = ap(o["out"])
        if kind == "memset":
            x = q.memset(out, o["val"])
        elif kind == "tt":
            x = q.tensor_tensor(out, ap(o["a"]), ap(o["b"]), o["op"])
        elif kind == "ts" or (kind == "either" and e == "V"):
            s1 = ap(o["s1"]) if isinstance(o["s1"], tuple) else o["s1"]
            if o["op1"] is None:
                x = q.tensor_scalar(out, ap(o["a"]), s1, None, o["op0"])
            else:
                x = q.tensor_scalar(out, ap(o["a"]), s1, o["s2"], o["op0"], o["op1"])
        elif kind == "vcopy" or (kind == "ecopy" and e == "V"):
            x = q.tensor_copy(out, ap(o["a"]))
        elif kind == "ecopy":
            x = q.activation(out, ap(o["a"]), AF.Copy)
        elif kind == "act" or kind == "either":
            x = q.activation(out, ap(o["a"]), o["func"], bias=o["bias"], scale=o["scale"])
        elif kind == "scan":
            x = q.tensor_tensor_scan(out, ap(o["d0"]), ap(o["d1"]), 0.0, o["op0"], o["op1"])
        elif kind == "red":
            x = q.tensor_reduce(out, ap(o["a"]), AxisListType.X, A.max)
        elif kind == "gather":
            src = ap(o["win"]).indirect(ap(o["off"]))
            x = q.tensor_copy(out, src) if e == "V" else q.activation(out, src, AF.Copy)
        elif kind == "mm":
            x = q.matmul(out, ap(o["lhs"]), ap(o["rhs"]), o["start"], o["stop"])
        elif kind == "asel":
            x = q.affine_select(out, ap(o["in_"]), o["pat"], o["op"], 0.0, o["base"], o["cm"])
        else:
            x = q.iota(out, [[0, o["out"][2]]], o["val"], 0, allow_small_or_imprecise_dtypes=True)
        x.then_inc(T.sem[s], 1)
    for s, val in pl["tail"]:
        g.wait_ge(T.sem[s], val)
